import numpy as np
import ml_dtypes


def mxq(x, axis, fmt="e4m3"):
    dtype, down = {"e4m3": (ml_dtypes.float8_e4m3fn, 7), "e5m2": (ml_dtypes.float8_e5m2, 14)}[fmt]
    v = np.moveaxis(np.asarray(x, np.float32).astype(ml_dtypes.bfloat16).astype(np.float64), axis, -1)
    blocks = v.reshape(v.shape[:-1] + (-1, 32))
    amax = np.abs(blocks).max(-1, keepdims=True)
    byte = np.maximum(np.where(amax > 0, np.frexp(amax)[1] - 1 + 127, 0) - down, 1)
    scale = np.exp2(byte - 127.0)
    codes = (blocks / scale).astype(np.float32).astype(dtype).astype(np.float64)
    return np.moveaxis((codes * scale).reshape(v.shape), -1, axis)


WIDE = False


def mx_kscale(k):
    if not WIDE:
        return np.ones(k)
    levels = np.array([10, -10, 5, -5, 0])
    if k % 512:
        return np.exp2(np.random.permutation(np.resize(levels, k // 32))).repeat(32)
    a = np.empty((k // 512, 16))
    for p in range(k // 512):
        a[p, :8] = np.random.permutation(np.resize(levels, 8))
        for g in range(8):
            far = levels[np.abs(levels - a[p, g]) >= 10]
            a[p, g + 8] = far[np.random.randint(len(far))]
    return np.exp2(a.ravel()).repeat(32)


def f64(x):
    return np.asarray(x).astype(np.float64)


def striped(idx):
    return np.tile(idx.reshape(-1, 16).T, (8, 1)).astype(np.uint16)


def unstriped(offs):
    return offs[:16].T.reshape(-1).astype(np.int64)


E2M1 = np.array([0.0, 0.5, 1.0, 1.5, 2.0, 3.0, 4.0, 6.0, -0.0, -0.5, -1.0, -1.5, -2.0, -3.0, -4.0, -6.0])


def pack_weight(w, fmt):
    k, n = w.shape
    w = f64(np.asarray(w, np.float32).astype(ml_dtypes.bfloat16)).reshape(k // 32, 32, n)
    amax = np.abs(w).max(1)
    if fmt == "e4m3":
        byte = np.frexp(amax)[1] - 1 + 127 - 7
    else:
        mant, ex = np.frexp(amax / 6.0)
        byte = np.where(mant > 0.5, ex, ex - 1) + 127
    byte = np.clip(np.where(amax > 0, byte, 1), 1, 254)
    scaled = (w * np.exp2(127.0 - byte)[:, None, :]).reshape(k, n).astype(np.float32)
    by_word = np.ascontiguousarray(scaled.reshape(k // 512, 128, 4, n).transpose(0, 1, 3, 2))
    if fmt == "e4m3":
        words = by_word.astype(ml_dtypes.float8_e4m3fn).view(np.uint8)
    else:
        c = by_word.astype(ml_dtypes.float4_e2m1fn).view(np.uint8) & 0xF
        words = (c[..., 0::2] | (c[..., 1::2] << 4)).reshape(k // 512, 128, 2 * n)
    return np.ascontiguousarray(words), np.ascontiguousarray(byte.astype(np.uint8).reshape(k // 512, 16, n))


def unpack_weight(words, scales, fmt):
    g, _, n = scales.shape
    words = np.ascontiguousarray(words).reshape(g, 128, n, -1)
    if fmt == "e4m3":
        vals = words.view(ml_dtypes.float8_e4m3fn).astype(np.float64)
    else:
        nib = np.empty((g, 128, n, 4), np.uint8)
        nib[..., 0::2] = words & 0xF
        nib[..., 1::2] = words >> 4
        vals = E2M1[nib]
    vals = vals * np.repeat(np.exp2(scales.astype(np.float64) - 127.0), 8, axis=1)[..., None]
    return vals.transpose(0, 1, 3, 2).reshape(g * 512, n)


def gelu(v):
    return 0.5 * v * (1.0 + np.tanh(np.sqrt(2.0 / np.pi) * (v + 0.044715 * v**3)))


K, H, T, S, T2, P = 1536, 512, 4096, 1024, 2048, 1024

def setup_inputs():
    n = np.random.standard_normal
    s, u = mx_kscale(K)[:, None], mx_kscale(H)[:, None]
    d = {}
    d["tab_words"], d["tab_scales"] = pack_weight(n((K, T)) * s, "e4m3")
    d["offs"] = striped(np.random.permutation(T)[:S])
    d["w1"] = (n((K, H)) * 2.0 / K ** 0.5 / s * u.T).astype(np.float32)
    d["lo"] = (-1.2 * np.exp(0.3 * n(H)) * u[:, 0]).astype(np.float32)
    d["hi"] = (1.6 * np.exp(0.3 * n(H)) * u[:, 0]).astype(np.float32)
    d["wgs"] = np.exp(0.3 * n((128, S))).astype(np.float32)
    d["page0"] = (1.5 * n((H, T2)) * u).astype(np.float32)
    d["offs2"] = striped(np.random.permutation(T2)[:S])
    d["sc"] = (np.exp(0.3 * n(H)) / u[:, 0]).astype(np.float32)
    d["offs3"] = striped(np.random.permutation(T2)[:P])
    d["gx"] = (np.exp(0.3 * n(H)) * u[:, 0]).astype(np.float32)
    d["w2_words"], d["w2_scales"] = pack_weight(n((H, H)) * 1.3 / H ** 0.5 / u * u.T, "e2m1")
    d["zone"] = (0.9 * n((H, P)) * u).astype(np.float32)
    d["w3"] = (n((H, H)) * 0.8 / H ** 0.5 / u).astype(np.float32)
    d["offs4"] = striped(np.random.permutation(T2)[:P])
    return d

def reference(tab_words, tab_scales, offs, w1, lo, hi, wgs, page0, offs2, sc, offs3, gx, w2_words, w2_scales, zone, w3, offs4):
    v = unpack_weight(tab_words, tab_scales, "e4m3")[:, unstriped(offs)]
    code = mxq(f64(w1), 0, "e4m3").T @ v
    h = np.minimum(np.maximum(code, f64(lo)[:, None]), f64(hi)[:, None])
    page = f64(page0).copy()
    page[:, unstriped(offs2)] = np.tile(f64(wgs), (H // 128, 1)) * h
    page = page * f64(sc)[:, None]
    x = f64(gx)[:, None] * np.tanh(page[:, unstriped(offs3)])
    w2 = unpack_weight(w2_words, w2_scales, "e2m1")
    b = (w2.T @ mxq(x, 0, "e4m3")) + f64(zone)
    y = mxq(f64(w3), 0, "e4m3").T @ mxq(b, 0, "e4m3")
    return y * page[:, unstriped(offs4)]

@@ -1,0 +1,298 @@
+from contextlib import ExitStack
+
+import concourse.mybir as mybir
+from concourse.masks import make_identity
+
+K, H, T, S, T2 = 1536, 512, 4096, 1024, 2048
+FLOPS = 2 * K * H * S + 2 * 2 * H * H * S
+
+F32 = mybir.dt.float32
+BF16 = mybir.dt.bfloat16
+I32 = mybir.dt.int32
+U32 = mybir.dt.uint32
+U16 = mybir.dt.uint16
+U8 = mybir.dt.uint8
+E4M3 = mybir.dt.float8_e4m3fn_x4
+E2M1 = mybir.dt.float4_e2m1fn_x4
+ALU = mybir.AluOpType
+ACT = mybir.ActivationFunctionType
+
+P = 128
+PACK = 4
+PASSES = K // (P * PACK)
+TILES = H // P
+HALF = 512
+HALVES = S // HALF
+LIST_COLS = HALF // 16
+
+
+def tile_list_brush_panel_features_kernel(
+    tc, tab_words, tab_scales, offs, w1, lo, hi, wgs, page0, offs2, sc, offs3, gx, w2_words, w2_scales, zone, w3, offs4, out
+):
+    nc = tc.nc
+    with ExitStack() as ctx:
+        lists = ctx.enter_context(tc.tile_pool(name="lists", bufs=1))
+        sb = ctx.enter_context(tc.tile_pool(name="sb", bufs=1))
+        psum = ctx.enter_context(tc.psum_pool(name="psum", bufs=1))
+
+        def load_list(src, name):
+            tile = lists.tile([P, S // 16], U16, name=name)
+            nc.sync.dma_start(tile[:], src)
+            return tile
+
+        def half_list(tile, half):
+            return tile[:, half * LIST_COLS : (half + 1) * LIST_COLS]
+
+        def half_cols(half):
+            return slice(half * HALF, (half + 1) * HALF)
+
+        tab_planes = sb.tile([P, T], U8, align_bytes=64)
+        nc.vector.memset(tab_planes[:].bitcast(I32), 0)
+        w2_raw_plane = sb.tile([P, H], U8, align_bytes=64)
+        nc.vector.memset(w2_raw_plane[:].bitcast(I32), 0)
+        bound_rows = sb.tile([P, P], F32)
+        nc.vector.memset(bound_rows[:], 0.0)
+        scale_rows = sb.tile([P, P], F32)
+        nc.vector.memset(scale_rows[:], 0.0)
+        ident_f32 = sb.tile([P, P], F32)
+        make_identity(nc, ident_f32[:])
+        ident_bf16 = sb.tile([P, P], BF16)
+        make_identity(nc, ident_bf16[:])
+
+        def load_table(a):
+            tile = sb.tile([P, T], I32, name=f"table{a}", tag=f"big{a}", align_bytes=64)
+            nc.sync.dma_start(out=tile[:], in_=tab_words[a].rearrange("p t i -> p (t i)").bitcast(I32))
+            return tile
+
+        def load_w1(t):
+            tiles = []
+            for a in range(PASSES):
+                raw = sb.tile([P, PACK, P], F32, name="w1_raw", bufs=2 * PASSES)
+                rows = w1[a * P * PACK : (a + 1) * P * PACK, t * P : (t + 1) * P]
+                nc.sync.dma_start(out=raw[:], in_=rows.rearrange("(p i) c -> p i c", i=PACK))
+                tiles.append(raw)
+            return tiles
+
+        def load_page(t):
+            tile = sb.tile([P, T2], F32, name=f"page{t}")
+            nc.sync.dma_start(out=tile[:], in_=page0[t * P : (t + 1) * P, :])
+            return tile
+
+        def load_rows(rows, first, second):
+            for v, src in enumerate((first, second)):
+                nc.sync.dma_start(out=rows[TILES * v : TILES * (v + 1), :], in_=src.rearrange("(t p) -> t p", p=P))
+
+        list1 = load_list(offs, "list1")
+        plane_rows = sb.tile([P, T // 4], I32, align_bytes=64)
+        for q in range(4):
+            live = slice(32 * q, 32 * q + 4 * PASSES)
+            nc.sync.dma_start(out=plane_rows[live, :], in_=tab_scales.bitcast(I32)[:, 4 * q : 4 * q + 4, :])
+            nc.vector.tensor_copy(tab_planes[live, :].bitcast(I32), plane_rows[live, :])
+        tables = [load_table(0)]
+        w2_raw = sb.tile([P, 2 * H], U8, align_bytes=64)
+        nc.sync.dma_start(out=w2_raw[:].bitcast(I32), in_=w2_words[0].bitcast(I32))
+        tables.append(load_table(1))
+        for q in range(4):
+            nc.sync.dma_start(
+                out=w2_raw_plane[32 * q : 32 * q + 4, :].bitcast(I32), in_=w2_scales[0].bitcast(I32)[4 * q : 4 * q + 4, :]
+            )
+        tables.append(load_table(2))
+        load_rows(bound_rows, lo, hi)
+        list2 = load_list(offs2, "list2")
+        w1_raw = [load_w1(0)]
+        gain = sb.tile([P, S], F32, tag="late")
+        nc.sync.dma_start(out=gain[:, half_cols(0)], in_=wgs[:, half_cols(0)])
+        pages = [load_page(0)]
+        w1_raw.append(load_w1(1))
+        nc.sync.dma_start(out=gain[:, half_cols(1)], in_=wgs[:, half_cols(1)])
+        pages.append(load_page(1))
+
+        def onto_partitions(rows, name):
+            bank = psum.tile([P, P], F32, name="rows_bank", tag="turn2", bufs=2)
+            nc.tensor.transpose(bank[:], rows[:], ident_f32[:])
+            columns = sb.tile([P, 2 * TILES], F32, name=name)
+            nc.scalar.copy(columns[:], bank[:, : 2 * TILES])
+            return [[columns[:, TILES * v + t : TILES * v + t + 1] for t in range(TILES)] for v in range(2)]
+
+        lo_col, hi_col = onto_partitions(bound_rows, "bound_columns")
+
+        v_planes = sb.tile([P, S], U8, align_bytes=64)
+        v_words = []
+        for a in range(PASSES):
+            words = sb.tile([P, S], U32, name=f"v_words{a}", tag=f"mid{a}", align_bytes=64)
+            v_words.append(words)
+        nc.vector.tensor_copy(v_planes[:], tab_planes[:].indirect(list1[:]))
+
+        def gather_words(a):
+            nc.vector.tensor_copy(v_words[a][:], tables[a][:].bitcast(U32).indirect(list1[:]))
+
+        gather_words(0)
+        gather_words(1)
+
+        def stage_w1(t):
+            staged = sb.tile([P, PASSES * P * PACK], BF16, name=f"w1_bf16_{t}", tag=f"stage{t}", align_bytes=64)
+            for a in range(PASSES):
+                nc.scalar.copy(
+                    staged[:, a * P * PACK : (a + 1) * P * PACK].rearrange("p (c i) -> p c i", i=PACK),
+                    w1_raw[t][a][:].rearrange("p i c -> p c i"),
+                )
+            return staged
+
+        def quantize_w1(t, staged):
+            codes = sb.tile([P, PASSES * P], U32, name=f"w1_codes{t}", align_bytes=64)
+            plane = sb.tile([P, PASSES * P], U8, name=f"w1_plane{t}", align_bytes=64)
+            for first, last in ((0, 2 * P), (2 * P, 3 * P)):
+                nc.vector.quantize_mx(
+                    out=codes[:, first:last].bitcast(E4M3), scales=plane[:, first:last], in_=staged[:, PACK * first : PACK * last]
+                )
+            return codes, plane
+
+        w2_codes = sb.tile([P, 2 * H], U8, align_bytes=64)
+        nc.vector.tensor_copy(
+            w2_codes[:].rearrange("p (i q e) -> p i q e", i=PACK, e=2), w2_raw[:].rearrange("p (q i e) -> p i q e", i=PACK, e=2)
+        )
+        w2_plane = sb.tile([P, H], U8, align_bytes=64)
+        nc.vector.tensor_copy(w2_plane[:].rearrange("p (i q) -> p i q", i=PACK), w2_raw_plane[:].rearrange("p (q i) -> p i q", i=PACK))
+
+        gather_words(2)
+        w1_quant = [quantize_w1(0, stage_w1(0))]
+
+        def first_product(t, half):
+            codes, plane = w1_quant[t]
+            bank = psum.tile([P, HALF], F32, name="code_bank", tag="acc", bufs=3)
+            for a in range(PASSES):
+                nc.tensor.matmul_mx(
+                    out=bank[:],
+                    lhsT=codes[:, a * P : (a + 1) * P].bitcast(E4M3),
+                    lhsT_scale=plane[:, a * P : (a + 1) * P],
+                    rhs=v_words[a][:, half_cols(half)].bitcast(E4M3),
+                    rhs_scale=v_planes[4 * a :, half_cols(half)],
+                    start=(a == 0),
+                    stop=(a == PASSES - 1),
+                )
+            code = sb.tile([P, HALF], F32, name="code", bufs=4)
+            nc.scalar.copy(code[:], bank[:])
+            return code
+
+        def bound_and_put(t, half, code, tag):
+            held = sb.tile([P, HALF], F32, name=f"held{t}_{half}", tag=tag, align_bytes=64)
+            nc.vector.tensor_scalar(held[:], code[:], lo_col[t], hi_col[t], ALU.max, ALU.min)
+            nc.vector.tensor_tensor(pages[t][:].indirect(half_list(list2, half)), held[:], gain[:, half_cols(half)], ALU.mult)
+
+        for t in range(TILES):
+            codes_t = [first_product(t, half) for half in range(HALVES)]
+            bound_and_put(t, 0, codes_t[0], f"held{t % 2}")
+            if t + 1 < TILES:
+                w1_quant.append(quantize_w1(t + 1, stage_w1(t + 1)))
+            if t + 2 < TILES:
+                w1_raw.append(load_w1(t + 2))
+                pages.append(load_page(t + 2))
+            bound_and_put(t, 1, codes_t[1], f"stage{t + 1}")
+
+        load_rows(scale_rows, sc, gx)
+        list3 = load_list(offs3, "list3")
+        w3_raw = sb.tile([P, PACK, H], F32)
+        nc.sync.dma_start(out=w3_raw[:], in_=w3.rearrange("(p i) n -> p i n", i=PACK))
+        zone_raw = sb.tile([P, PACK, S], F32, tag="big0", align_bytes=64)
+        nc.sync.dma_start(out=zone_raw[:], in_=zone.rearrange("(p i) j -> p i j", i=PACK))
+        list4 = load_list(offs4, "list4")
+
+        sc_col, gx_col = onto_partitions(scale_rows, "scale_columns")
+        w3_bf16 = sb.tile([P, H * PACK], BF16, align_bytes=64)
+        nc.scalar.copy(w3_bf16[:].rearrange("p (n i) -> p n i", i=PACK), w3_raw[:].rearrange("p i n -> p n i"))
+        w3_codes = sb.tile([P, H], U32, align_bytes=64)
+        w3_plane = sb.tile([P, H], U8, align_bytes=64)
+        nc.vector.quantize_mx(out=w3_codes[:].bitcast(E4M3), scales=w3_plane[:], in_=w3_bf16[:])
+
+        zone_woven = sb.tile([P, S * PACK], F32, tag="big1", align_bytes=64)
+        for half in range(HALVES):
+            nc.scalar.copy(
+                zone_woven[:, half * HALF * PACK : (half + 1) * HALF * PACK].rearrange("p (j i) -> p j i", i=PACK),
+                zone_raw[:, :, half_cols(half)].rearrange("p i j -> p j i"),
+            )
+
+        picked = sb.tile([P, HALVES * TILES * HALF], F32, tag="late")
+        squashed = sb.tile([P, HALVES * TILES * HALF], F32, tag="big0", align_bytes=64)
+
+        def piece(half, t):
+            return slice((half * TILES + t) * HALF, (half * TILES + t + 1) * HALF)
+
+        for half in range(HALVES):
+            for t in range(TILES):
+                nc.vector.tensor_copy(picked[:, piece(half, t)], pages[t][:].indirect(half_list(list3, half)))
+
+        def make_x(half):
+            turned = sb.tile([P, HALF // P, H], BF16, name=f"x_turned{half}", tag=("big2", "x_turned1")[half], align_bytes=64)
+            for t in range(TILES):
+                nc.scalar.activation(squashed[:, piece(half, t)], picked[:, piece(half, t)], ACT.Tanh, scale=sc_col[t])
+                x_rows = sb.tile([P, HALF], BF16, name="x_rows", bufs=3)
+                nc.scalar.activation(x_rows[:], squashed[:, piece(half, t)], ACT.Copy, scale=gx_col[t])
+                bank = psum.tile([P, HALF // P, P], BF16, name="turn1", tag="turn1")
+                for c in range(HALF // P):
+                    nc.tensor.transpose(bank[:, c, :], x_rows[:, c * P : (c + 1) * P], ident_bf16[:])
+                nc.scalar.copy(turned[:, :, t * P : (t + 1) * P], bank[:])
+            woven = sb.tile([P, HALF * PACK], BF16, name=f"x_woven{half}", tag=("mid2", "x_woven1")[half], align_bytes=64)
+            pairs = turned[:].rearrange("p c r -> p (c r)").bitcast(F32)
+            for cc in range(HALF // (2 * P)):
+                bank = psum.tile([P, 2, 2, P], F32, name="turn2", tag="turn2", bufs=2)
+                for c in range(2):
+                    first = (2 * cc + c) * 2 * P
+                    for u in range(2):
+                        nc.tensor.transpose(bank[:, c, u, :], pairs[:, first + u : first + 2 * P : 2], ident_f32[:])
+                nc.scalar.copy(
+                    woven[:].bitcast(F32)[:, cc * HALF : (cc + 1) * HALF].rearrange("p (c j u) -> p c j u", c=2, u=2),
+                    bank[:].rearrange("p c u j -> p c j u"),
+                )
+            return woven
+
+        def quantize_half(woven, name):
+            codes = sb.tile([P, HALF], U32, name=f"{name}_codes", align_bytes=64)
+            plane = sb.tile([P, HALF], U8, name=f"{name}_plane", align_bytes=64)
+            nc.vector.quantize_mx(out=codes[:].bitcast(E4M3), scales=plane[:], in_=woven[:])
+            return codes, plane
+
+        def make_b(half, x_codes, x_plane):
+            woven = sb.tile([P, HALF * PACK], BF16, name=f"b_woven{half}", tag=f"mid{half}", align_bytes=64)
+            for c in range(HALF // P):
+                bank = psum.tile([P, PACK, P], F32, name="b_bank", tag="b_bank", bufs=2)
+                for i in range(PACK):
+                    nc.tensor.matmul_mx(
+                        out=bank[:, i, :],
+                        lhsT=w2_codes[:, 2 * i * P : 2 * (i + 1) * P].bitcast(E2M1),
+                        lhsT_scale=w2_plane[:, i * P : (i + 1) * P],
+                        rhs=x_codes[:, c * P : (c + 1) * P].bitcast(E4M3),
+                        rhs_scale=x_plane[:, c * P : (c + 1) * P],
+                        start=True,
+                        stop=True,
+                    )
+                first = (half * HALF + c * P) * PACK
+                nc.vector.tensor_tensor(
+                    woven[:, c * P * PACK : (c + 1) * P * PACK].rearrange("p (j i) -> p j i", i=PACK),
+                    bank[:].rearrange("p i j -> p j i"),
+                    zone_woven[:, first : first + P * PACK].rearrange("p (j i) -> p j i", i=PACK),
+                    ALU.add,
+                )
+            return woven
+
+        def finish(half, b_codes, b_plane):
+            for t in range(TILES):
+                bank = psum.tile([P, HALF], F32, name="y_bank", tag="acc", bufs=3)
+                nc.tensor.matmul_mx(
+                    out=bank[:],
+                    lhsT=w3_codes[:, t * P : (t + 1) * P].bitcast(E4M3),
+                    lhsT_scale=w3_plane[:, t * P : (t + 1) * P],
+                    rhs=b_codes[:].bitcast(E4M3),
+                    rhs_scale=b_plane[:],
+                    start=True,
+                    stop=True,
+                )
+                scaled = sb.tile([P, HALF], F32, name="scaled", bufs=3)
+                nc.scalar.activation(scaled[:], bank[:], ACT.Copy, scale=sc_col[t])
+                result = sb.tile([P, HALF], F32, name="result", bufs=3)
+                nc.vector.tensor_tensor(result[:], pages[t][:].indirect(half_list(list4, half)), scaled[:], ALU.mult)
+                nc.sync.dma_start(out=out[t * P : (t + 1) * P, half_cols(half)], in_=result[:])
+
+        for half in range(HALVES):
+            x_codes, x_plane = quantize_half(make_x(half), f"x{half}")
+            b_codes, b_plane = quantize_half(make_b(half, x_codes, x_plane), f"b{half}")
+            finish(half, b_codes, b_plane)

@@ -47,13 +47,23 @@ def tile_list_brush_panel_features_kernel(
             return slice(half * HALF, (half + 1) * HALF)
 
         tab_planes = sb.tile([P, T], U8, align_bytes=64)
-        nc.vector.memset(tab_planes[:].bitcast(I32), 0)
+        nc.gpsimd.memset(tab_planes[:].bitcast(I32), 0)
+        for q in range(4):
+            nc.gpsimd.dma_start(
+                out=tab_planes[32 * q : 32 * q + 4 * PASSES, :].bitcast(I32), in_=tab_scales.bitcast(I32)[:, 4 * q : 4 * q + 4, :]
+            )
         w2_raw_plane = sb.tile([P, H], U8, align_bytes=64)
         nc.vector.memset(w2_raw_plane[:].bitcast(I32), 0)
         bound_rows = sb.tile([P, P], F32)
         nc.vector.memset(bound_rows[:], 0.0)
         scale_rows = sb.tile([P, P], F32)
         nc.vector.memset(scale_rows[:], 0.0)
+        w2_raw = sb.tile([P, 2 * H], U8, align_bytes=64)
+        nc.gpsimd.dma_start(out=w2_raw[:].bitcast(I32), in_=w2_words[0].bitcast(I32))
+        for q in range(4):
+            nc.gpsimd.dma_start(
+                out=w2_raw_plane[32 * q : 32 * q + 4, :].bitcast(I32), in_=w2_scales[0].bitcast(I32)[4 * q : 4 * q + 4, :]
+            )
         ident_f32 = sb.tile([P, P], F32)
         make_identity(nc, ident_f32[:])
         ident_bf16 = sb.tile([P, P], BF16)
@@ -67,7 +77,7 @@ def tile_list_brush_panel_features_kernel(
         def load_w1(t):
             tiles = []
             for a in range(PASSES):
-                raw = sb.tile([P, PACK, P], F32, name="w1_raw", bufs=2 * PASSES)
+                raw = sb.tile([P, PACK, P], F32, name=f"w1_raw{t}_{a}", tag=f"raw{t % 2}_{a}")
                 rows = w1[a * P * PACK : (a + 1) * P * PACK, t * P : (t + 1) * P]
                 nc.sync.dma_start(out=raw[:], in_=rows.rearrange("(p i) c -> p i c", i=PACK))
                 tiles.append(raw)
@@ -78,34 +88,24 @@ def tile_list_brush_panel_features_kernel(
             nc.sync.dma_start(out=tile[:], in_=page0[t * P : (t + 1) * P, :])
             return tile
 
-        def load_rows(rows, first, second):
+        def load_rows(queue, rows, first, second):
             for v, src in enumerate((first, second)):
-                nc.sync.dma_start(out=rows[TILES * v : TILES * (v + 1), :], in_=src.rearrange("(t p) -> t p", p=P))
+                queue.dma_start(out=rows[TILES * v : TILES * (v + 1), :], in_=src.rearrange("(t p) -> t p", p=P))
 
         list1 = load_list(offs, "list1")
-        plane_rows = sb.tile([P, T // 4], I32, align_bytes=64)
-        for q in range(4):
-            live = slice(32 * q, 32 * q + 4 * PASSES)
-            nc.sync.dma_start(out=plane_rows[live, :], in_=tab_scales.bitcast(I32)[:, 4 * q : 4 * q + 4, :])
-            nc.vector.tensor_copy(tab_planes[live, :].bitcast(I32), plane_rows[live, :])
-        tables = [load_table(0)]
-        w2_raw = sb.tile([P, 2 * H], U8, align_bytes=64)
-        nc.sync.dma_start(out=w2_raw[:].bitcast(I32), in_=w2_words[0].bitcast(I32))
-        tables.append(load_table(1))
-        for q in range(4):
-            nc.sync.dma_start(
-                out=w2_raw_plane[32 * q : 32 * q + 4, :].bitcast(I32), in_=w2_scales[0].bitcast(I32)[4 * q : 4 * q + 4, :]
-            )
-        tables.append(load_table(2))
-        load_rows(bound_rows, lo, hi)
-        list2 = load_list(offs2, "list2")
+        tables = [load_table(0), load_table(1)]
         w1_raw = [load_w1(0)]
+        tables.append(load_table(2))
+        list2 = load_list(offs2, "list2")
+        load_rows(nc.scalar, bound_rows, lo, hi)
         gain = sb.tile([P, S], F32, tag="late")
         nc.sync.dma_start(out=gain[:, half_cols(0)], in_=wgs[:, half_cols(0)])
         pages = [load_page(0)]
         w1_raw.append(load_w1(1))
         nc.sync.dma_start(out=gain[:, half_cols(1)], in_=wgs[:, half_cols(1)])
         pages.append(load_page(1))
+        load_rows(nc.sync, scale_rows, sc, gx)
+        list3 = load_list(offs3, "list3")
 
         def onto_partitions(rows, name):
             bank = psum.tile([P, P], F32, name="rows_bank", tag="turn2", bufs=2)
@@ -154,8 +154,10 @@ def tile_list_brush_panel_features_kernel(
         w2_plane = sb.tile([P, H], U8, align_bytes=64)
         nc.vector.tensor_copy(w2_plane[:].rearrange("p (i q) -> p i q", i=PACK), w2_raw_plane[:].rearrange("p (q i) -> p i q", i=PACK))
 
-        gather_words(2)
         w1_quant = [quantize_w1(0, stage_w1(0))]
+        last = PASSES - 1
+        for half in range(HALVES):
+            nc.vector.tensor_copy(v_words[last][:, half_cols(half)], tables[last][:].bitcast(U32).indirect(half_list(list1, half)))
 
         def first_product(t, half):
             codes, plane = w1_quant[t]
@@ -170,6 +172,8 @@ def tile_list_brush_panel_features_kernel(
                     start=(a == 0),
                     stop=(a == PASSES - 1),
                 )
+            if t == 0 and half == 0:
+                return bank
             code = sb.tile([P, HALF], F32, name="code", bufs=4)
             nc.scalar.copy(code[:], bank[:])
             return code
@@ -179,60 +183,23 @@ def tile_list_brush_panel_features_kernel(
             nc.vector.tensor_scalar(held[:], code[:], lo_col[t], hi_col[t], ALU.max, ALU.min)
             nc.vector.tensor_tensor(pages[t][:].indirect(half_list(list2, half)), held[:], gain[:, half_cols(half)], ALU.mult)
 
-        for t in range(TILES):
-            codes_t = [first_product(t, half) for half in range(HALVES)]
-            bound_and_put(t, 0, codes_t[0], f"held{t % 2}")
-            if t + 1 < TILES:
-                w1_quant.append(quantize_w1(t + 1, stage_w1(t + 1)))
-            if t + 2 < TILES:
-                w1_raw.append(load_w1(t + 2))
-                pages.append(load_page(t + 2))
-            bound_and_put(t, 1, codes_t[1], f"stage{t + 1}")
+        def pick(t, half, tag, bufs):
+            picked = sb.tile([P, HALF], F32, name=f"picked{t}_{half}", tag=tag, bufs=bufs)
+            nc.vector.tensor_copy(picked[:], pages[t][:].indirect(half_list(list3, half)))
+            return picked
 
-        load_rows(scale_rows, sc, gx)
-        list3 = load_list(offs3, "list3")
-        w3_raw = sb.tile([P, PACK, H], F32)
-        nc.sync.dma_start(out=w3_raw[:], in_=w3.rearrange("(p i) n -> p i n", i=PACK))
-        zone_raw = sb.tile([P, PACK, S], F32, tag="big0", align_bytes=64)
-        nc.sync.dma_start(out=zone_raw[:], in_=zone.rearrange("(p i) j -> p i j", i=PACK))
-        list4 = load_list(offs4, "list4")
+        def make_rows(t, half, picked, squashed):
+            nc.scalar.activation(squashed, picked[:], ACT.Tanh, scale=sc_col[t])
+            x_rows = sb.tile([P, HALF], BF16, name="x_rows", bufs=3)
+            nc.scalar.activation(x_rows[:], squashed, ACT.Copy, scale=gx_col[t])
+            bank = psum.tile([P, HALF // P, P], BF16, name="turn1", tag="turn1")
+            for c in range(HALF // P):
+                nc.tensor.transpose(bank[:, c, :], x_rows[:, c * P : (c + 1) * P], ident_bf16[:])
+            nc.scalar.copy(turned[half][:, :, t * P : (t + 1) * P], bank[:])
 
-        sc_col, gx_col = onto_partitions(scale_rows, "scale_columns")
-        w3_bf16 = sb.tile([P, H * PACK], BF16, align_bytes=64)
-        nc.scalar.copy(w3_bf16[:].rearrange("p (n i) -> p n i", i=PACK), w3_raw[:].rearrange("p i n -> p n i"))
-        w3_codes = sb.tile([P, H], U32, align_bytes=64)
-        w3_plane = sb.tile([P, H], U8, align_bytes=64)
-        nc.vector.quantize_mx(out=w3_codes[:].bitcast(E4M3), scales=w3_plane[:], in_=w3_bf16[:])
-
-        zone_woven = sb.tile([P, S * PACK], F32, tag="big1", align_bytes=64)
-        for half in range(HALVES):
-            nc.scalar.copy(
-                zone_woven[:, half * HALF * PACK : (half + 1) * HALF * PACK].rearrange("p (j i) -> p j i", i=PACK),
-                zone_raw[:, :, half_cols(half)].rearrange("p i j -> p j i"),
-            )
-
-        picked = sb.tile([P, HALVES * TILES * HALF], F32, tag="late")
-        squashed = sb.tile([P, HALVES * TILES * HALF], F32, tag="big0", align_bytes=64)
-
-        def piece(half, t):
-            return slice((half * TILES + t) * HALF, (half * TILES + t + 1) * HALF)
-
-        for half in range(HALVES):
-            for t in range(TILES):
-                nc.vector.tensor_copy(picked[:, piece(half, t)], pages[t][:].indirect(half_list(list3, half)))
-
-        def make_x(half):
-            turned = sb.tile([P, HALF // P, H], BF16, name=f"x_turned{half}", tag=("big2", "x_turned1")[half], align_bytes=64)
-            for t in range(TILES):
-                nc.scalar.activation(squashed[:, piece(half, t)], picked[:, piece(half, t)], ACT.Tanh, scale=sc_col[t])
-                x_rows = sb.tile([P, HALF], BF16, name="x_rows", bufs=3)
-                nc.scalar.activation(x_rows[:], squashed[:, piece(half, t)], ACT.Copy, scale=gx_col[t])
-                bank = psum.tile([P, HALF // P, P], BF16, name="turn1", tag="turn1")
-                for c in range(HALF // P):
-                    nc.tensor.transpose(bank[:, c, :], x_rows[:, c * P : (c + 1) * P], ident_bf16[:])
-                nc.scalar.copy(turned[:, :, t * P : (t + 1) * P], bank[:])
+        def weave_x(half):
             woven = sb.tile([P, HALF * PACK], BF16, name=f"x_woven{half}", tag=("mid2", "x_woven1")[half], align_bytes=64)
-            pairs = turned[:].rearrange("p c r -> p (c r)").bitcast(F32)
+            pairs = turned[half][:].rearrange("p c r -> p (c r)").bitcast(F32)
             for cc in range(HALF // (2 * P)):
                 bank = psum.tile([P, 2, 2, P], F32, name="turn2", tag="turn2", bufs=2)
                 for c in range(2):
@@ -244,6 +211,59 @@ def tile_list_brush_panel_features_kernel(
                     bank[:].rearrange("p c u j -> p c j u"),
                 )
             return woven
+
+        turned = []
+        for half in range(HALVES):
+            tile = sb.tile([P, HALF // P, H], BF16, name=f"x_turned{half}", tag=("big2", "x_turned1")[half], align_bytes=64)
+            turned.append(tile)
+
+        staged = None
+        for t in range(TILES):
+            codes_t = [first_product(t, half) for half in range(HALVES)]
+            if t + 1 < TILES:
+                staged = stage_w1(t + 1)
+            if t == 1:
+                sc_col, gx_col = onto_partitions(scale_rows, "scale_columns")
+            if t == TILES - 1:
+                w3_bf16 = sb.tile([P, H * PACK], BF16, align_bytes=64)
+                nc.scalar.copy(w3_bf16[:].rearrange("p (n i) -> p n i", i=PACK), w3_raw[:].rearrange("p i n -> p n i"))
+                zone_woven = sb.tile([P, S * PACK], F32, tag="big1", align_bytes=64)
+                for half in range(HALVES):
+                    nc.scalar.copy(
+                        zone_woven[:, half * HALF * PACK : (half + 1) * HALF * PACK].rearrange("p (j i) -> p j i", i=PACK),
+                        zone_raw[:, :, half_cols(half)].rearrange("p i j -> p j i"),
+                    )
+                squashed_late = sb.tile([P, 4 * HALF], F32, tag="big0", align_bytes=64)
+                make_rows(t - 1, 0, pick(t - 1, 0, "picked", 3), squashed_late[:, :HALF])
+            elif t > 0:
+                for half in range(HALVES):
+                    squashed = sb.tile([P, HALF], F32, name=f"squashed{t - 1}_{half}", tag=f"raw{t - 1}_{PASSES - 1 - half}")
+                    make_rows(t - 1, half, pick(t - 1, half, "picked", 3), squashed[:])
+            bound_and_put(t, 0, codes_t[0], f"held{t % 2}")
+            if t + 1 < TILES:
+                w1_quant.append(quantize_w1(t + 1, staged))
+            else:
+                w3_codes = sb.tile([P, H], U32, align_bytes=64)
+                w3_plane = sb.tile([P, H], U8, align_bytes=64)
+                nc.vector.quantize_mx(out=w3_codes[:].bitcast(E4M3), scales=w3_plane[:], in_=w3_bf16[:])
+            if t + 2 < TILES:
+                w1_raw.append(load_w1(t + 2))
+                pages.append(load_page(t + 2))
+            if t + 2 == TILES - 1:
+                w3_raw = sb.tile([P, PACK, H], F32)
+                nc.sync.dma_start(out=w3_raw[:], in_=w3.rearrange("(p i) n -> p i n", i=PACK))
+                zone_raw = sb.tile([P, PACK, S], F32, tag="big0", align_bytes=64)
+                nc.sync.dma_start(out=zone_raw[:], in_=zone.rearrange("(p i) j -> p i j", i=PACK))
+                list4 = load_list(offs4, "list4")
+            bound_and_put(t, 1, codes_t[1], f"stage{t + 1}")
+
+        late = [(3, 0, "picked", 3), (2, 1, "late", 1), (3, 1, "picked", 3)]
+        late_picked = [pick(*piece) for piece in late]
+        x_woven = []
+        for n, (t, half, tag, bufs) in enumerate(late):
+            make_rows(t, half, late_picked[n], squashed_late[:, (n + 1) * HALF : (n + 2) * HALF])
+            if t == TILES - 1:
+                x_woven.append(weave_x(half))
 
         def quantize_half(woven, name):
             codes = sb.tile([P, HALF], U32, name=f"{name}_codes", align_bytes=64)
@@ -274,7 +294,8 @@ def tile_list_brush_panel_features_kernel(
                 )
             return woven
 
-        def finish(half, b_codes, b_plane):
+        def third_product(b_codes, b_plane):
+            tiles = []
             for t in range(TILES):
                 bank = psum.tile([P, HALF], F32, name="y_bank", tag="acc", bufs=3)
                 nc.tensor.matmul_mx(
@@ -286,13 +307,19 @@ def tile_list_brush_panel_features_kernel(
                     start=True,
                     stop=True,
                 )
-                scaled = sb.tile([P, HALF], F32, name="scaled", bufs=3)
+                scaled = sb.tile([P, HALF], F32, name="scaled", bufs=8)
                 nc.scalar.activation(scaled[:], bank[:], ACT.Copy, scale=sc_col[t])
-                result = sb.tile([P, HALF], F32, name="result", bufs=3)
-                nc.vector.tensor_tensor(result[:], pages[t][:].indirect(half_list(list4, half)), scaled[:], ALU.mult)
-                nc.sync.dma_start(out=out[t * P : (t + 1) * P, half_cols(half)], in_=result[:])
+                tiles.append(scaled)
+            return tiles
+
+        scaled_y = []
+        for half in range(HALVES):
+            x_codes, x_plane = quantize_half(x_woven[half], f"x{half}")
+            b_codes, b_plane = quantize_half(make_b(half, x_codes, x_plane), f"b{half}")
+            scaled_y.append(third_product(b_codes, b_plane))
 
         for half in range(HALVES):
-            x_codes, x_plane = quantize_half(make_x(half), f"x{half}")
-            b_codes, b_plane = quantize_half(make_b(half, x_codes, x_plane), f"b{half}")
-            finish(half, b_codes, b_plane)
+            for t in range(TILES):
+                result = sb.tile([P, HALF], F32, name="result", bufs=3)
+                nc.vector.tensor_tensor(result[:], pages[t][:].indirect(half_list(list4, half)), scaled_y[half][t][:], ALU.mult)
+                nc.sync.dma_start(out=out[t * P : (t + 1) * P, half_cols(half)], in_=result[:])

@@ -54,16 +54,8 @@ def tile_list_brush_panel_features_kernel(
             )
         w2_raw_plane = sb.tile([P, H], U8, align_bytes=64)
         nc.vector.memset(w2_raw_plane[:].bitcast(I32), 0)
-        bound_rows = sb.tile([P, P], F32)
-        nc.vector.memset(bound_rows[:], 0.0)
-        scale_rows = sb.tile([P, P], F32)
-        nc.vector.memset(scale_rows[:], 0.0)
-        w2_raw = sb.tile([P, 2 * H], U8, align_bytes=64)
-        nc.gpsimd.dma_start(out=w2_raw[:].bitcast(I32), in_=w2_words[0].bitcast(I32))
-        for q in range(4):
-            nc.gpsimd.dma_start(
-                out=w2_raw_plane[32 * q : 32 * q + 4, :].bitcast(I32), in_=w2_scales[0].bitcast(I32)[4 * q : 4 * q + 4, :]
-            )
+        channel_rows = sb.tile([P, P], F32)
+        nc.vector.memset(channel_rows[:], 0.0)
         ident_f32 = sb.tile([P, P], F32)
         make_identity(nc, ident_f32[:])
         ident_bf16 = sb.tile([P, P], BF16)
@@ -77,7 +69,7 @@ def tile_list_brush_panel_features_kernel(
         def load_w1(t):
             tiles = []
             for a in range(PASSES):
-                raw = sb.tile([P, PACK, P], F32, name=f"w1_raw{t}_{a}", tag=f"raw{t % 2}_{a}")
+                raw = sb.tile([P, PACK, P], F32, name=f"w1_raw{t}_{a}", tag=f"raw{t}_{a}")
                 rows = w1[a * P * PACK : (a + 1) * P * PACK, t * P : (t + 1) * P]
                 nc.sync.dma_start(out=raw[:], in_=rows.rearrange("(p i) c -> p i c", i=PACK))
                 tiles.append(raw)
@@ -88,45 +80,38 @@ def tile_list_brush_panel_features_kernel(
             nc.sync.dma_start(out=tile[:], in_=page0[t * P : (t + 1) * P, :])
             return tile
 
-        def load_rows(queue, rows, first, second):
-            for v, src in enumerate((first, second)):
-                queue.dma_start(out=rows[TILES * v : TILES * (v + 1), :], in_=src.rearrange("(t p) -> t p", p=P))
-
         list1 = load_list(offs, "list1")
         tables = [load_table(0), load_table(1)]
         w1_raw = [load_w1(0)]
         tables.append(load_table(2))
         list2 = load_list(offs2, "list2")
-        load_rows(nc.scalar, bound_rows, lo, hi)
+        for v, src in enumerate((lo, hi, sc, gx)):
+            nc.scalar.dma_start(out=channel_rows[TILES * v : TILES * (v + 1), :], in_=src.rearrange("(t p) -> t p", p=P))
         gain = sb.tile([P, S], F32, tag="late")
         nc.sync.dma_start(out=gain[:, half_cols(0)], in_=wgs[:, half_cols(0)])
         pages = [load_page(0)]
         w1_raw.append(load_w1(1))
         nc.sync.dma_start(out=gain[:, half_cols(1)], in_=wgs[:, half_cols(1)])
-        pages.append(load_page(1))
-        load_rows(nc.sync, scale_rows, sc, gx)
-        list3 = load_list(offs3, "list3")
 
-        def onto_partitions(rows, name):
-            bank = psum.tile([P, P], F32, name="rows_bank", tag="turn2", bufs=2)
-            nc.tensor.transpose(bank[:], rows[:], ident_f32[:])
-            columns = sb.tile([P, 2 * TILES], F32, name=name)
-            nc.scalar.copy(columns[:], bank[:, : 2 * TILES])
-            return [[columns[:, TILES * v + t : TILES * v + t + 1] for t in range(TILES)] for v in range(2)]
-
-        lo_col, hi_col = onto_partitions(bound_rows, "bound_columns")
+        channel_bank = psum.tile([P, P], F32, tag="turn2", bufs=2)
+        nc.tensor.transpose(channel_bank[:], channel_rows[:], ident_f32[:])
+        channel_columns = sb.tile([P, 4 * TILES], F32)
+        nc.scalar.copy(channel_columns[:], channel_bank[:, : 4 * TILES])
+        lo_col, hi_col, sc_col, gx_col = [
+            [channel_columns[:, TILES * v + t : TILES * v + t + 1] for t in range(TILES)] for v in range(4)
+        ]
 
         v_planes = sb.tile([P, S], U8, align_bytes=64)
         v_words = []
         for a in range(PASSES):
             words = sb.tile([P, S], U32, name=f"v_words{a}", tag=f"mid{a}", align_bytes=64)
             v_words.append(words)
-        nc.vector.tensor_copy(v_planes[:], tab_planes[:].indirect(list1[:]))
 
         def gather_words(a):
             nc.vector.tensor_copy(v_words[a][:], tables[a][:].bitcast(U32).indirect(list1[:]))
 
         gather_words(0)
+        nc.vector.tensor_copy(v_planes[:], tab_planes[:].indirect(list1[:]))
         gather_words(1)
 
         def stage_w1(t):
@@ -139,7 +124,7 @@ def tile_list_brush_panel_features_kernel(
             return staged
 
         def quantize_w1(t, staged):
-            codes = sb.tile([P, PASSES * P], U32, name=f"w1_codes{t}", align_bytes=64)
+            codes = sb.tile([P, PASSES * P], U32, name=f"w1_codes{t}", tag=("codes0", "held0", "held1", "stage2")[t], align_bytes=64)
             plane = sb.tile([P, PASSES * P], U8, name=f"w1_plane{t}", align_bytes=64)
             for first, last in ((0, 2 * P), (2 * P, 3 * P)):
                 nc.vector.quantize_mx(
@@ -147,14 +132,10 @@ def tile_list_brush_panel_features_kernel(
                 )
             return codes, plane
 
-        w2_codes = sb.tile([P, 2 * H], U8, align_bytes=64)
-        nc.vector.tensor_copy(
-            w2_codes[:].rearrange("p (i q e) -> p i q e", i=PACK, e=2), w2_raw[:].rearrange("p (q i e) -> p i q e", i=PACK, e=2)
-        )
-        w2_plane = sb.tile([P, H], U8, align_bytes=64)
-        nc.vector.tensor_copy(w2_plane[:].rearrange("p (i q) -> p i q", i=PACK), w2_raw_plane[:].rearrange("p (q i) -> p i q", i=PACK))
-
         w1_quant = [quantize_w1(0, stage_w1(0))]
+        w1_raw.append(load_w1(2))
+        pages.append(load_page(1))
+        list3 = load_list(offs3, "list3")
         last = PASSES - 1
         for half in range(HALVES):
             nc.vector.tensor_copy(v_words[last][:, half_cols(half)], tables[last][:].bitcast(U32).indirect(half_list(list1, half)))
@@ -172,30 +153,34 @@ def tile_list_brush_panel_features_kernel(
                     start=(a == 0),
                     stop=(a == PASSES - 1),
                 )
-            if t == 0 and half == 0:
-                return bank
-            code = sb.tile([P, HALF], F32, name="code", bufs=4)
-            nc.scalar.copy(code[:], bank[:])
-            return code
+            return bank
 
-        def bound_and_put(t, half, code, tag):
-            held = sb.tile([P, HALF], F32, name=f"held{t}_{half}", tag=tag, align_bytes=64)
-            nc.vector.tensor_scalar(held[:], code[:], lo_col[t], hi_col[t], ALU.max, ALU.min)
-            nc.vector.tensor_tensor(pages[t][:].indirect(half_list(list2, half)), held[:], gain[:, half_cols(half)], ALU.mult)
+        def bound(t, code, tag):
+            held = sb.tile([P, code.shape[1]], F32, name=f"held{t}", tag=tag, align_bytes=64)
+            nc.vector.tensor_scalar(held[:], code, lo_col[t], hi_col[t], ALU.max, ALU.min)
+            return held
 
-        def pick(t, half, tag, bufs):
-            picked = sb.tile([P, HALF], F32, name=f"picked{t}_{half}", tag=tag, bufs=bufs)
-            nc.vector.tensor_copy(picked[:], pages[t][:].indirect(half_list(list3, half)))
+        def put(t, held, offsets, cols):
+            nc.vector.tensor_tensor(pages[t][:].indirect(offsets), held[:], gain[:, cols], ALU.mult)
+
+        def pick(t, offsets, tag):
+            picked = sb.tile([P, 16 * offsets.shape[1]], F32, name=f"picked{t}", tag=tag)
+            nc.vector.tensor_copy(picked[:], pages[t][:].indirect(offsets))
             return picked
 
         def make_rows(t, half, picked, squashed):
-            nc.scalar.activation(squashed, picked[:], ACT.Tanh, scale=sc_col[t])
+            nc.scalar.activation(squashed, picked, ACT.Tanh, scale=sc_col[t])
             x_rows = sb.tile([P, HALF], BF16, name="x_rows", bufs=3)
             nc.scalar.activation(x_rows[:], squashed, ACT.Copy, scale=gx_col[t])
             bank = psum.tile([P, HALF // P, P], BF16, name="turn1", tag="turn1")
             for c in range(HALF // P):
                 nc.tensor.transpose(bank[:, c, :], x_rows[:, c * P : (c + 1) * P], ident_bf16[:])
             nc.scalar.copy(turned[half][:, :, t * P : (t + 1) * P], bank[:])
+
+        def make_early_rows(t, picked, block):
+            for half in range(HALVES):
+                squashed = sb.tile([P, HALF], F32, name=f"squashed{t}_{half}", tag=f"raw{block}_{PASSES - 1 - half}")
+                make_rows(t, half, picked[:, half_cols(half)], squashed[:])
 
         def weave_x(half):
             woven = sb.tile([P, HALF * PACK], BF16, name=f"x_woven{half}", tag=("mid2", "x_woven1")[half], align_bytes=64)
@@ -217,58 +202,80 @@ def tile_list_brush_panel_features_kernel(
             tile = sb.tile([P, HALF // P, H], BF16, name=f"x_turned{half}", tag=("big2", "x_turned1")[half], align_bytes=64)
             turned.append(tile)
 
-        staged = None
-        for t in range(TILES):
-            codes_t = [first_product(t, half) for half in range(HALVES)]
+        banks = [first_product(0, half) for half in range(HALVES)]
+        code = sb.tile([P, HALF], F32, name="code0", tag="code0")
+        nc.scalar.copy(code[:], banks[1][:])
+        staged = stage_w1(1)
+        put(0, bound(0, banks[0][:], "held0"), half_list(list2, 0), half_cols(0))
+        held = bound(0, code[:], "held1")
+        w1_quant.append(quantize_w1(1, staged))
+        put(0, held, half_list(list2, 1), half_cols(1))
+
+        w1_raw.append(load_w1(3))
+        pages.extend([load_page(2), load_page(3)])
+        w3_raw = sb.tile([P, PACK, H], F32)
+        nc.sync.dma_start(out=w3_raw[:], in_=w3.rearrange("(p i) n -> p i n", i=PACK))
+        zone_raw = sb.tile([P, PACK, S], F32, tag="big1", align_bytes=64)
+        nc.sync.dma_start(out=zone_raw[:], in_=zone.rearrange("(p i) j -> p i j", i=PACK))
+        w2_raw = sb.tile([P, 2 * H], U8, align_bytes=64)
+        nc.sync.dma_start(out=w2_raw[:].bitcast(I32), in_=w2_words[0].bitcast(I32))
+        for q in range(4):
+            nc.sync.dma_start(
+                out=w2_raw_plane[32 * q : 32 * q + 4, :].bitcast(I32), in_=w2_scales[0].bitcast(I32)[4 * q : 4 * q + 4, :]
+            )
+        list4 = load_list(offs4, "list4")
+
+        for t in range(1, TILES):
+            code = sb.tile([P, S], F32, name=f"code{t}", tag=("stage3", "w3_bf16", "code3")[t - 1], align_bytes=64)
+            for half in range(HALVES):
+                nc.scalar.copy(code[:, half_cols(half)], first_product(t, half)[:])
             if t + 1 < TILES:
-                staged = stage_w1(t + 1)
+                w1_quant.append(quantize_w1(t + 1, stage_w1(t + 1)))
+            held = bound(t, code[:], f"stage{t + 1}")
             if t == 1:
-                sc_col, gx_col = onto_partitions(scale_rows, "scale_columns")
-            if t == TILES - 1:
-                w3_bf16 = sb.tile([P, H * PACK], BF16, align_bytes=64)
+                picked = pick(0, list3[:], "picked")
+            elif t == 2:
+                make_early_rows(0, picked, 3)
+                make_early_rows(1, pick(1, list3[:], "picked"), 2)
+            else:
+                w3_bf16 = sb.tile([P, H * PACK], BF16, tag="w3_bf16", align_bytes=64)
                 nc.scalar.copy(w3_bf16[:].rearrange("p (n i) -> p n i", i=PACK), w3_raw[:].rearrange("p i n -> p n i"))
-                zone_woven = sb.tile([P, S * PACK], F32, tag="big1", align_bytes=64)
+                zone_woven = sb.tile([P, S * PACK], F32, tag="stage2", align_bytes=64)
                 for half in range(HALVES):
                     nc.scalar.copy(
                         zone_woven[:, half * HALF * PACK : (half + 1) * HALF * PACK].rearrange("p (j i) -> p j i", i=PACK),
                         zone_raw[:, :, half_cols(half)].rearrange("p i j -> p j i"),
                     )
-                squashed_late = sb.tile([P, 4 * HALF], F32, tag="big0", align_bytes=64)
-                make_rows(t - 1, 0, pick(t - 1, 0, "picked", 3), squashed_late[:, :HALF])
-            elif t > 0:
-                for half in range(HALVES):
-                    squashed = sb.tile([P, HALF], F32, name=f"squashed{t - 1}_{half}", tag=f"raw{t - 1}_{PASSES - 1 - half}")
-                    make_rows(t - 1, half, pick(t - 1, half, "picked", 3), squashed[:])
-            bound_and_put(t, 0, codes_t[0], f"held{t % 2}")
-            if t + 1 < TILES:
-                w1_quant.append(quantize_w1(t + 1, staged))
-            else:
-                w3_codes = sb.tile([P, H], U32, align_bytes=64)
-                w3_plane = sb.tile([P, H], U8, align_bytes=64)
-                nc.vector.quantize_mx(out=w3_codes[:].bitcast(E4M3), scales=w3_plane[:], in_=w3_bf16[:])
-            if t + 2 < TILES:
-                w1_raw.append(load_w1(t + 2))
-                pages.append(load_page(t + 2))
-            if t + 2 == TILES - 1:
-                w3_raw = sb.tile([P, PACK, H], F32)
-                nc.sync.dma_start(out=w3_raw[:], in_=w3.rearrange("(p i) n -> p i n", i=PACK))
-                zone_raw = sb.tile([P, PACK, S], F32, tag="big0", align_bytes=64)
-                nc.sync.dma_start(out=zone_raw[:], in_=zone.rearrange("(p i) j -> p i j", i=PACK))
-                list4 = load_list(offs4, "list4")
-            bound_and_put(t, 1, codes_t[1], f"stage{t + 1}")
+                squashed_late = sb.tile([P, 4 * HALF], F32, tag="big1", align_bytes=64)
+                make_rows(t - 1, 0, pick(t - 1, half_list(list3, 0), "picked")[:], squashed_late[:, :HALF])
+            put(t, held, list2[:], slice(0, S))
 
-        late = [(3, 0, "picked", 3), (2, 1, "late", 1), (3, 1, "picked", 3)]
-        late_picked = [pick(*piece) for piece in late]
+        late = [(3, 0, "code0"), (2, 1, "late"), (3, 1, "picked_last")]
+        late_picked = [pick(t, half_list(list3, half), tag) for t, half, tag in late]
+        late_bytes = sb.tile([P, 8 * H], U8, tag=f"stage{TILES}", align_bytes=64)
+        w2_codes, w2_plane = late_bytes[:, : 2 * H], late_bytes[:, 2 * H : 3 * H]
+        w3_plane, w3_codes = late_bytes[:, 3 * H : 4 * H], late_bytes[:, 4 * H :].bitcast(U32)
+        nc.vector.tensor_copy(
+            w2_codes.rearrange("p (i q e) -> p i q e", i=PACK, e=2), w2_raw[:].rearrange("p (q i e) -> p i q e", i=PACK, e=2)
+        )
+        nc.vector.tensor_copy(w2_plane.rearrange("p (i q) -> p i q", i=PACK), w2_raw_plane[:].rearrange("p (q i) -> p i q", i=PACK))
+        nc.vector.quantize_mx(out=w3_codes.bitcast(E4M3), scales=w3_plane, in_=w3_bf16[:])
         x_woven = []
-        for n, (t, half, tag, bufs) in enumerate(late):
-            make_rows(t, half, late_picked[n], squashed_late[:, (n + 1) * HALF : (n + 2) * HALF])
+        for n, (t, half, tag) in enumerate(late):
+            make_rows(t, half, late_picked[n][:], squashed_late[:, (n + 1) * HALF : (n + 2) * HALF])
             if t == TILES - 1:
                 x_woven.append(weave_x(half))
 
-        def quantize_half(woven, name):
+        def quantize_half(woven, name, calls):
             codes = sb.tile([P, HALF], U32, name=f"{name}_codes", align_bytes=64)
             plane = sb.tile([P, HALF], U8, name=f"{name}_plane", align_bytes=64)
-            nc.vector.quantize_mx(out=codes[:].bitcast(E4M3), scales=plane[:], in_=woven[:])
+            width = HALF // calls
+            for first in range(0, HALF, width):
+                nc.vector.quantize_mx(
+                    out=codes[:, first : first + width].bitcast(E4M3),
+                    scales=plane[:, first : first + width],
+                    in_=woven[:, PACK * first : PACK * (first + width)],
+                )
             return codes, plane
 
         def make_b(half, x_codes, x_plane):
@@ -294,8 +301,9 @@ def tile_list_brush_panel_features_kernel(
                 )
             return woven
 
-        def third_product(b_codes, b_plane):
-            tiles = []
+        scaled = sb.tile([P, HALVES * TILES, HALF], F32, tag="big0", align_bytes=64)
+
+        def third_product(half, b_codes, b_plane):
             for t in range(TILES):
                 bank = psum.tile([P, HALF], F32, name="y_bank", tag="acc", bufs=3)
                 nc.tensor.matmul_mx(
@@ -307,19 +315,15 @@ def tile_list_brush_panel_features_kernel(
                     start=True,
                     stop=True,
                 )
-                scaled = sb.tile([P, HALF], F32, name="scaled", bufs=8)
-                nc.scalar.activation(scaled[:], bank[:], ACT.Copy, scale=sc_col[t])
-                tiles.append(scaled)
-            return tiles
+                nc.scalar.activation(scaled[:, half * TILES + t, :], bank[:], ACT.Copy, scale=sc_col[t])
 
-        scaled_y = []
         for half in range(HALVES):
-            x_codes, x_plane = quantize_half(x_woven[half], f"x{half}")
-            b_codes, b_plane = quantize_half(make_b(half, x_codes, x_plane), f"b{half}")
-            scaled_y.append(third_product(b_codes, b_plane))
+            x_codes, x_plane = quantize_half(x_woven[half], f"x{half}", 2)
+            b_codes, b_plane = quantize_half(make_b(half, x_codes, x_plane), f"b{half}", 1)
+            third_product(half, b_codes, b_plane)
 
         for half in range(HALVES):
             for t in range(TILES):
                 result = sb.tile([P, HALF], F32, name="result", bufs=3)
-                nc.vector.tensor_tensor(result[:], pages[t][:].indirect(half_list(list4, half)), scaled_y[half][t][:], ALU.mult)
+                nc.vector.tensor_tensor(result[:], pages[t][:].indirect(half_list(list4, half)), scaled[:, half * TILES + t, :], ALU.mult)
                 nc.sync.dma_start(out=out[t * P : (t + 1) * P, half_cols(half)], in_=result[:])

@@ -24,6 +24,7 @@ TILES = H // P
 HALF = 512
 HALVES = S // HALF
 LIST_COLS = HALF // 16
+RUN = 4
 
 
 def tile_list_brush_panel_features_kernel(
@@ -111,20 +112,20 @@ def tile_list_brush_panel_features_kernel(
             nc.vector.tensor_copy(v_words[a][:], tables[a][:].bitcast(U32).indirect(list1[:]))
 
         gather_words(0)
-        nc.vector.tensor_copy(v_planes[:], tab_planes[:].indirect(list1[:]))
         gather_words(1)
+        nc.vector.tensor_copy(v_planes[:], tab_planes[:].indirect(list1[:]))
 
         def stage_w1(t):
             staged = sb.tile([P, PASSES * P * PACK], BF16, name=f"w1_bf16_{t}", tag=f"stage{t}", align_bytes=64)
             for a in range(PASSES):
                 nc.scalar.copy(
-                    staged[:, a * P * PACK : (a + 1) * P * PACK].rearrange("p (c i) -> p c i", i=PACK),
-                    w1_raw[t][a][:].rearrange("p i c -> p c i"),
+                    staged[:, a * P * PACK : (a + 1) * P * PACK].rearrange("p (c e i) -> p c i e", e=RUN, i=PACK),
+                    w1_raw[t][a][:].rearrange("p i (c e) -> p c i e", e=RUN),
                 )
             return staged
 
         def quantize_w1(t, staged):
-            codes = sb.tile([P, PASSES * P], U32, name=f"w1_codes{t}", tag=("codes0", "held0", "held1", "stage2")[t], align_bytes=64)
+            codes = sb.tile([P, PASSES * P], U32, name=f"w1_codes{t}", tag=("codes0", "held0", "stage1", "stage2")[t], align_bytes=64)
             plane = sb.tile([P, PASSES * P], U8, name=f"w1_plane{t}", align_bytes=64)
             for first, last in ((0, 2 * P), (2 * P, 3 * P)):
                 nc.vector.quantize_mx(
@@ -175,7 +176,10 @@ def tile_list_brush_panel_features_kernel(
             bank = psum.tile([P, HALF // P, P], BF16, name="turn1", tag="turn1")
             for c in range(HALF // P):
                 nc.tensor.transpose(bank[:, c, :], x_rows[:, c * P : (c + 1) * P], ident_bf16[:])
-            nc.scalar.copy(turned[half][:, :, t * P : (t + 1) * P], bank[:])
+            nc.scalar.copy(
+                turned[half][:, :, :, t * P // PACK : (t + 1) * P // PACK],
+                bank[:].rearrange("p c r -> p (c r)").bitcast(F32).rearrange("p (c q u) -> p c u q", c=HALF // P, u=2),
+            )
 
         def make_early_rows(t, picked, block):
             for half in range(HALVES):
@@ -184,13 +188,11 @@ def tile_list_brush_panel_features_kernel(
 
         def weave_x(half):
             woven = sb.tile([P, HALF * PACK], BF16, name=f"x_woven{half}", tag=("mid2", "x_woven1")[half], align_bytes=64)
-            pairs = turned[half][:].rearrange("p c r -> p (c r)").bitcast(F32)
             for cc in range(HALF // (2 * P)):
                 bank = psum.tile([P, 2, 2, P], F32, name="turn2", tag="turn2", bufs=2)
                 for c in range(2):
-                    first = (2 * cc + c) * 2 * P
                     for u in range(2):
-                        nc.tensor.transpose(bank[:, c, u, :], pairs[:, first + u : first + 2 * P : 2], ident_f32[:])
+                        nc.tensor.transpose(bank[:, c, u, :], turned[half][:, 2 * cc + c, u, :], ident_f32[:])
                 nc.scalar.copy(
                     woven[:].bitcast(F32)[:, cc * HALF : (cc + 1) * HALF].rearrange("p (c j u) -> p c j u", c=2, u=2),
                     bank[:].rearrange("p c u j -> p c j u"),
@@ -199,7 +201,7 @@ def tile_list_brush_panel_features_kernel(
 
         turned = []
         for half in range(HALVES):
-            tile = sb.tile([P, HALF // P, H], BF16, name=f"x_turned{half}", tag=("big2", "x_turned1")[half], align_bytes=64)
+            tile = sb.tile([P, HALF // P, 2, P], F32, name=f"x_turned{half}", tag=("big2", "x_turned1")[half], align_bytes=64)
             turned.append(tile)
 
         banks = [first_product(0, half) for half in range(HALVES)]
@@ -207,9 +209,8 @@ def tile_list_brush_panel_features_kernel(
         nc.scalar.copy(code[:], banks[1][:])
         staged = stage_w1(1)
         put(0, bound(0, banks[0][:], "held0"), half_list(list2, 0), half_cols(0))
-        held = bound(0, code[:], "held1")
         w1_quant.append(quantize_w1(1, staged))
-        put(0, held, half_list(list2, 1), half_cols(1))
+        put(0, bound(0, code[:], "stage1"), half_list(list2, 1), half_cols(1))
 
         w1_raw.append(load_w1(3))
         pages.extend([load_page(2), load_page(3)])
@@ -236,18 +237,20 @@ def tile_list_brush_panel_features_kernel(
                 picked = pick(0, list3[:], "picked")
             elif t == 2:
                 make_early_rows(0, picked, 3)
-                make_early_rows(1, pick(1, list3[:], "picked"), 2)
+                make_early_rows(1, pick(1, list3[:], "picked1"), 2)
             else:
                 w3_bf16 = sb.tile([P, H * PACK], BF16, tag="w3_bf16", align_bytes=64)
-                nc.scalar.copy(w3_bf16[:].rearrange("p (n i) -> p n i", i=PACK), w3_raw[:].rearrange("p i n -> p n i"))
+                nc.scalar.copy(
+                    w3_bf16[:].rearrange("p (c e i) -> p c i e", e=RUN, i=PACK), w3_raw[:].rearrange("p i (c e) -> p c i e", e=RUN)
+                )
                 zone_woven = sb.tile([P, S * PACK], F32, tag="stage2", align_bytes=64)
                 for half in range(HALVES):
                     nc.scalar.copy(
-                        zone_woven[:, half * HALF * PACK : (half + 1) * HALF * PACK].rearrange("p (j i) -> p j i", i=PACK),
-                        zone_raw[:, :, half_cols(half)].rearrange("p i j -> p j i"),
+                        zone_woven[:, half * HALF * PACK : (half + 1) * HALF * PACK].rearrange("p (c e i) -> p c i e", e=RUN, i=PACK),
+                        zone_raw[:, :, half_cols(half)].rearrange("p i (c e) -> p c i e", e=RUN),
                     )
                 squashed_late = sb.tile([P, 4 * HALF], F32, tag="big1", align_bytes=64)
-                make_rows(t - 1, 0, pick(t - 1, half_list(list3, 0), "picked")[:], squashed_late[:, :HALF])
+                make_rows(t - 1, 0, pick(t - 1, half_list(list3, 0), "picked2")[:], squashed_late[:, :HALF])
             put(t, held, list2[:], slice(0, S))
 
         late = [(3, 0, "code0"), (2, 1, "late"), (3, 1, "picked_last")]

from contextlib import ExitStack

import concourse.mybir as mybir
from concourse.masks import make_identity

K, H, T, S, T2 = 1536, 512, 4096, 1024, 2048
FLOPS = 2 * K * H * S + 2 * 2 * H * H * S

F32 = mybir.dt.float32
BF16 = mybir.dt.bfloat16
I32 = mybir.dt.int32
U32 = mybir.dt.uint32
U16 = mybir.dt.uint16
U8 = mybir.dt.uint8
E4M3 = mybir.dt.float8_e4m3fn_x4
E2M1 = mybir.dt.float4_e2m1fn_x4
ALU = mybir.AluOpType
ACT = mybir.ActivationFunctionType

P = 128
PACK = 4
PASSES = K // (P * PACK)
TILES = H // P
HALF = 512
HALVES = S // HALF
LIST_COLS = HALF // 16
RUN = 4


def tile_list_brush_panel_features_kernel(
    tc, tab_words, tab_scales, offs, w1, lo, hi, wgs, page0, offs2, sc, offs3, gx, w2_words, w2_scales, zone, w3, offs4, out
):
    nc = tc.nc
    with ExitStack() as ctx:
        lists = ctx.enter_context(tc.tile_pool(name="lists", bufs=1))
        sb = ctx.enter_context(tc.tile_pool(name="sb", bufs=1))
        psum = ctx.enter_context(tc.psum_pool(name="psum", bufs=1))

        def load_list(src, name):
            tile = lists.tile([P, S // 16], U16, name=name)
            nc.sync.dma_start(tile[:], src)
            return tile

        def half_list(tile, half):
            return tile[:, half * LIST_COLS : (half + 1) * LIST_COLS]

        def half_cols(half):
            return slice(half * HALF, (half + 1) * HALF)

        tab_planes = sb.tile([P, T], U8, align_bytes=64)
        nc.gpsimd.memset(tab_planes[:].bitcast(I32), 0)
        for q in range(4):
            nc.gpsimd.dma_start(
                out=tab_planes[32 * q : 32 * q + 4 * PASSES, :].bitcast(I32), in_=tab_scales.bitcast(I32)[:, 4 * q : 4 * q + 4, :]
            )
        w2_raw_plane = sb.tile([P, H], U8, align_bytes=64)
        nc.vector.memset(w2_raw_plane[:].bitcast(I32), 0)
        channel_rows = sb.tile([P, P], F32)
        nc.vector.memset(channel_rows[:], 0.0)
        ident_f32 = sb.tile([P, P], F32)
        make_identity(nc, ident_f32[:])
        ident_bf16 = sb.tile([P, P], BF16)
        make_identity(nc, ident_bf16[:])

        def load_table(a):
            tile = sb.tile([P, T], I32, name=f"table{a}", tag=f"big{a}", align_bytes=64)
            nc.sync.dma_start(out=tile[:], in_=tab_words[a].rearrange("p t i -> p (t i)").bitcast(I32))
            return tile

        def load_w1(t):
            tiles = []
            for a in range(PASSES):
                raw = sb.tile([P, PACK, P], F32, name=f"w1_raw{t}_{a}", tag=f"raw{t}_{a}")
                rows = w1[a * P * PACK : (a + 1) * P * PACK, t * P : (t + 1) * P]
                nc.sync.dma_start(out=raw[:], in_=rows.rearrange("(p i) c -> p i c", i=PACK))
                tiles.append(raw)
            return tiles

        def load_page(t):
            tile = sb.tile([P, T2], F32, name=f"page{t}")
            nc.sync.dma_start(out=tile[:], in_=page0[t * P : (t + 1) * P, :])
            return tile

        list1 = load_list(offs, "list1")
        tables = [load_table(0), load_table(1)]
        w1_raw = [load_w1(0)]
        tables.append(load_table(2))
        list2 = load_list(offs2, "list2")
        for v, src in enumerate((lo, hi, sc, gx)):
            nc.scalar.dma_start(out=channel_rows[TILES * v : TILES * (v + 1), :], in_=src.rearrange("(t p) -> t p", p=P))
        gain = sb.tile([P, S], F32, tag="late")
        nc.sync.dma_start(out=gain[:, half_cols(0)], in_=wgs[:, half_cols(0)])
        pages = [load_page(0)]
        w1_raw.append(load_w1(1))
        nc.sync.dma_start(out=gain[:, half_cols(1)], in_=wgs[:, half_cols(1)])

        channel_bank = psum.tile([P, P], F32, tag="turn2", bufs=2)
        nc.tensor.transpose(channel_bank[:], channel_rows[:], ident_f32[:])
        channel_columns = sb.tile([P, 4 * TILES], F32)
        nc.scalar.copy(channel_columns[:], channel_bank[:, : 4 * TILES])
        lo_col, hi_col, sc_col, gx_col = [
            [channel_columns[:, TILES * v + t : TILES * v + t + 1] for t in range(TILES)] for v in range(4)
        ]

        v_planes = sb.tile([P, S], U8, align_bytes=64)
        v_words = []
        for a in range(PASSES):
            words = sb.tile([P, S], U32, name=f"v_words{a}", tag=f"mid{a}", align_bytes=64)
            v_words.append(words)

        def gather_words(a):
            nc.vector.tensor_copy(v_words[a][:], tables[a][:].bitcast(U32).indirect(list1[:]))

        gather_words(0)
        gather_words(1)
        nc.vector.tensor_copy(v_planes[:], tab_planes[:].indirect(list1[:]))

        def stage_w1(t):
            staged = sb.tile([P, PASSES * P * PACK], BF16, name=f"w1_bf16_{t}", tag=f"stage{t}", align_bytes=64)
            for a in range(PASSES):
                nc.scalar.copy(
                    staged[:, a * P * PACK : (a + 1) * P * PACK].rearrange("p (c e i) -> p c i e", e=RUN, i=PACK),
                    w1_raw[t][a][:].rearrange("p i (c e) -> p c i e", e=RUN),
                )
            return staged

        def quantize_w1(t, staged):
            codes = sb.tile([P, PASSES * P], U32, name=f"w1_codes{t}", tag=("codes0", "held0", "stage1", "stage2")[t], align_bytes=64)
            plane = sb.tile([P, PASSES * P], U8, name=f"w1_plane{t}", align_bytes=64)
            for first, last in ((0, 2 * P), (2 * P, 3 * P)):
                nc.vector.quantize_mx(
                    out=codes[:, first:last].bitcast(E4M3), scales=plane[:, first:last], in_=staged[:, PACK * first : PACK * last]
                )
            return codes, plane

        w1_quant = [quantize_w1(0, stage_w1(0))]
        w1_raw.append(load_w1(2))
        pages.append(load_page(1))
        list3 = load_list(offs3, "list3")
        last = PASSES - 1
        for half in range(HALVES):
            nc.vector.tensor_copy(v_words[last][:, half_cols(half)], tables[last][:].bitcast(U32).indirect(half_list(list1, half)))

        def first_product(t, half):
            codes, plane = w1_quant[t]
            bank = psum.tile([P, HALF], F32, name="code_bank", tag="acc", bufs=3)
            for a in range(PASSES):
                nc.tensor.matmul_mx(
                    out=bank[:],
                    lhsT=codes[:, a * P : (a + 1) * P].bitcast(E4M3),
                    lhsT_scale=plane[:, a * P : (a + 1) * P],
                    rhs=v_words[a][:, half_cols(half)].bitcast(E4M3),
                    rhs_scale=v_planes[4 * a :, half_cols(half)],
                    start=(a == 0),
                    stop=(a == PASSES - 1),
                )
            return bank

        def bound(t, code, tag):
            held = sb.tile([P, code.shape[1]], F32, name=f"held{t}", tag=tag, align_bytes=64)
            nc.vector.tensor_scalar(held[:], code, lo_col[t], hi_col[t], ALU.max, ALU.min)
            return held

        def put(t, held, offsets, cols):
            nc.vector.tensor_tensor(pages[t][:].indirect(offsets), held[:], gain[:, cols], ALU.mult)

        def pick(t, offsets, tag):
            picked = sb.tile([P, 16 * offsets.shape[1]], F32, name=f"picked{t}", tag=tag)
            nc.vector.tensor_copy(picked[:], pages[t][:].indirect(offsets))
            return picked

        def make_rows(t, half, picked, squashed):
            nc.scalar.activation(squashed, picked, ACT.Tanh, scale=sc_col[t])
            x_rows = sb.tile([P, HALF], BF16, name="x_rows", bufs=3)
            nc.scalar.activation(x_rows[:], squashed, ACT.Copy, scale=gx_col[t])
            bank = psum.tile([P, HALF // P, P], BF16, name="turn1", tag="turn1")
            for c in range(HALF // P):
                nc.tensor.transpose(bank[:, c, :], x_rows[:, c * P : (c + 1) * P], ident_bf16[:])
            nc.scalar.copy(
                turned[half][:, :, :, t * P // PACK : (t + 1) * P // PACK],
                bank[:].rearrange("p c r -> p (c r)").bitcast(F32).rearrange("p (c q u) -> p c u q", c=HALF // P, u=2),
            )

        def make_early_rows(t, picked, block):
            for half in range(HALVES):
                squashed = sb.tile([P, HALF], F32, name=f"squashed{t}_{half}", tag=f"raw{block}_{PASSES - 1 - half}")
                make_rows(t, half, picked[:, half_cols(half)], squashed[:])

        def weave_x(half):
            woven = sb.tile([P, HALF * PACK], BF16, name=f"x_woven{half}", tag=("mid2", "x_woven1")[half], align_bytes=64)
            for cc in range(HALF // (2 * P)):
                bank = psum.tile([P, 2, 2, P], F32, name="turn2", tag="turn2", bufs=2)
                for c in range(2):
                    for u in range(2):
                        nc.tensor.transpose(bank[:, c, u, :], turned[half][:, 2 * cc + c, u, :], ident_f32[:])
                nc.scalar.copy(
                    woven[:].bitcast(F32)[:, cc * HALF : (cc + 1) * HALF].rearrange("p (c j u) -> p c j u", c=2, u=2),
                    bank[:].rearrange("p c u j -> p c j u"),
                )
            return woven

        turned = []
        for half in range(HALVES):
            tile = sb.tile([P, HALF // P, 2, P], F32, name=f"x_turned{half}", tag=("big2", "x_turned1")[half], align_bytes=64)
            turned.append(tile)

        banks = [first_product(0, half) for half in range(HALVES)]
        code = sb.tile([P, HALF], F32, name="code0", tag="code0")
        nc.scalar.copy(code[:], banks[1][:])
        staged = stage_w1(1)
        put(0, bound(0, banks[0][:], "held0"), half_list(list2, 0), half_cols(0))
        w1_quant.append(quantize_w1(1, staged))
        put(0, bound(0, code[:], "stage1"), half_list(list2, 1), half_cols(1))

        w1_raw.append(load_w1(3))
        pages.extend([load_page(2), load_page(3)])
        w3_raw = sb.tile([P, PACK, H], F32)
        nc.sync.dma_start(out=w3_raw[:], in_=w3.rearrange("(p i) n -> p i n", i=PACK))
        zone_raw = sb.tile([P, PACK, S], F32, tag="big1", align_bytes=64)
        nc.sync.dma_start(out=zone_raw[:], in_=zone.rearrange("(p i) j -> p i j", i=PACK))
        w2_raw = sb.tile([P, 2 * H], U8, align_bytes=64)
        nc.sync.dma_start(out=w2_raw[:].bitcast(I32), in_=w2_words[0].bitcast(I32))
        for q in range(4):
            nc.sync.dma_start(
                out=w2_raw_plane[32 * q : 32 * q + 4, :].bitcast(I32), in_=w2_scales[0].bitcast(I32)[4 * q : 4 * q + 4, :]
            )
        list4 = load_list(offs4, "list4")

        for t in range(1, TILES):
            code = sb.tile([P, S], F32, name=f"code{t}", tag=("stage3", "w3_bf16", "code3")[t - 1], align_bytes=64)
            for half in range(HALVES):
                nc.scalar.copy(code[:, half_cols(half)], first_product(t, half)[:])
            if t + 1 < TILES:
                w1_quant.append(quantize_w1(t + 1, stage_w1(t + 1)))
            held = bound(t, code[:], f"stage{t + 1}")
            if t == 1:
                picked = pick(0, list3[:], "picked")
            elif t == 2:
                make_early_rows(0, picked, 3)
                make_early_rows(1, pick(1, list3[:], "picked1"), 2)
            else:
                w3_bf16 = sb.tile([P, H * PACK], BF16, tag="w3_bf16", align_bytes=64)
                nc.scalar.copy(
                    w3_bf16[:].rearrange("p (c e i) -> p c i e", e=RUN, i=PACK), w3_raw[:].rearrange("p i (c e) -> p c i e", e=RUN)
                )
                zone_woven = sb.tile([P, S * PACK], F32, tag="stage2", align_bytes=64)
                for half in range(HALVES):
                    nc.scalar.copy(
                        zone_woven[:, half * HALF * PACK : (half + 1) * HALF * PACK].rearrange("p (c e i) -> p c i e", e=RUN, i=PACK),
                        zone_raw[:, :, half_cols(half)].rearrange("p i (c e) -> p c i e", e=RUN),
                    )
                squashed_late = sb.tile([P, 4 * HALF], F32, tag="big1", align_bytes=64)
                make_rows(t - 1, 0, pick(t - 1, half_list(list3, 0), "picked2")[:], squashed_late[:, :HALF])
            put(t, held, list2[:], slice(0, S))

        late = [(3, 0, "code0"), (2, 1, "late"), (3, 1, "picked_last")]
        late_picked = [pick(t, half_list(list3, half), tag) for t, half, tag in late]
        late_bytes = sb.tile([P, 8 * H], U8, tag=f"stage{TILES}", align_bytes=64)
        w2_codes, w2_plane = late_bytes[:, : 2 * H], late_bytes[:, 2 * H : 3 * H]
        w3_plane, w3_codes = late_bytes[:, 3 * H : 4 * H], late_bytes[:, 4 * H :].bitcast(U32)
        nc.vector.tensor_copy(
            w2_codes.rearrange("p (i q e) -> p i q e", i=PACK, e=2), w2_raw[:].rearrange("p (q i e) -> p i q e", i=PACK, e=2)
        )
        nc.vector.tensor_copy(w2_plane.rearrange("p (i q) -> p i q", i=PACK), w2_raw_plane[:].rearrange("p (q i) -> p i q", i=PACK))
        nc.vector.quantize_mx(out=w3_codes.bitcast(E4M3), scales=w3_plane, in_=w3_bf16[:])
        x_woven = []
        for n, (t, half, tag) in enumerate(late):
            make_rows(t, half, late_picked[n][:], squashed_late[:, (n + 1) * HALF : (n + 2) * HALF])
            if t == TILES - 1:
                x_woven.append(weave_x(half))

        def quantize_half(woven, name, calls):
            codes = sb.tile([P, HALF], U32, name=f"{name}_codes", align_bytes=64)
            plane = sb.tile([P, HALF], U8, name=f"{name}_plane", align_bytes=64)
            width = HALF // calls
            for first in range(0, HALF, width):
                nc.vector.quantize_mx(
                    out=codes[:, first : first + width].bitcast(E4M3),
                    scales=plane[:, first : first + width],
                    in_=woven[:, PACK * first : PACK * (first + width)],
                )
            return codes, plane

        def make_b(half, x_codes, x_plane):
            woven = sb.tile([P, HALF * PACK], BF16, name=f"b_woven{half}", tag=f"mid{half}", align_bytes=64)
            for c in range(HALF // P):
                bank = psum.tile([P, PACK, P], F32, name="b_bank", tag="b_bank", bufs=2)
                for i in range(PACK):
                    nc.tensor.matmul_mx(
                        out=bank[:, i, :],
                        lhsT=w2_codes[:, 2 * i * P : 2 * (i + 1) * P].bitcast(E2M1),
                        lhsT_scale=w2_plane[:, i * P : (i + 1) * P],
                        rhs=x_codes[:, c * P : (c + 1) * P].bitcast(E4M3),
                        rhs_scale=x_plane[:, c * P : (c + 1) * P],
                        start=True,
                        stop=True,
                    )
                first = (half * HALF + c * P) * PACK
                nc.vector.tensor_tensor(
                    woven[:, c * P * PACK : (c + 1) * P * PACK].rearrange("p (j i) -> p j i", i=PACK),
                    bank[:].rearrange("p i j -> p j i"),
                    zone_woven[:, first : first + P * PACK].rearrange("p (j i) -> p j i", i=PACK),
                    ALU.add,
                )
            return woven

        scaled = sb.tile([P, HALVES * TILES, HALF], F32, tag="big0", align_bytes=64)

        def third_product(half, b_codes, b_plane):
            for t in range(TILES):
                bank = psum.tile([P, HALF], F32, name="y_bank", tag="acc", bufs=3)
                nc.tensor.matmul_mx(
                    out=bank[:],
                    lhsT=w3_codes[:, t * P : (t + 1) * P].bitcast(E4M3),
                    lhsT_scale=w3_plane[:, t * P : (t + 1) * P],
                    rhs=b_codes[:].bitcast(E4M3),
                    rhs_scale=b_plane[:],
                    start=True,
                    stop=True,
                )
                nc.scalar.activation(scaled[:, half * TILES + t, :], bank[:], ACT.Copy, scale=sc_col[t])

        for half in range(HALVES):
            x_codes, x_plane = quantize_half(x_woven[half], f"x{half}", 2)
            b_codes, b_plane = quantize_half(make_b(half, x_codes, x_plane), f"b{half}", 1)
            third_product(half, b_codes, b_plane)

        for half in range(HALVES):
            for t in range(TILES):
                result = sb.tile([P, HALF], F32, name="result", bufs=3)
                nc.vector.tensor_tensor(result[:], pages[t][:].indirect(half_list(list4, half)), scaled[:, half * TILES + t, :], ALU.mult)
                nc.sync.dma_start(out=out[t * P : (t + 1) * P, half_cols(half)], in_=result[:])
